import numpy as np
import ml_dtypes


def mxq(x, axis, fmt="e4m3"):
    dtype, down = {"e4m3": (ml_dtypes.float8_e4m3fn, 7), "e5m2": (ml_dtypes.float8_e5m2, 14)}[fmt]
    v = np.moveaxis(np.asarray(x, np.float32).astype(ml_dtypes.bfloat16).astype(np.float64), axis, -1)
    blocks = v.reshape(v.shape[:-1] + (-1, 32))
    amax = np.abs(blocks).max(-1, keepdims=True)
    byte = np.maximum(np.where(amax > 0, np.frexp(amax)[1] - 1 + 127, 0) - down, 1)
    scale = np.exp2(byte - 127.0)
    codes = (blocks / scale).astype(np.float32).astype(dtype).astype(np.float64)
    return np.moveaxis((codes * scale).reshape(v.shape), -1, axis)


WIDE = False


def mx_kscale(k):
    if not WIDE:
        return np.ones(k)
    levels = np.array([10, -10, 5, -5, 0])
    if k % 512:
        return np.exp2(np.random.permutation(np.resize(levels, k // 32))).repeat(32)
    a = np.empty((k // 512, 16))
    for p in range(k // 512):
        a[p, :8] = np.random.permutation(np.resize(levels, 8))
        for g in range(8):
            far = levels[np.abs(levels - a[p, g]) >= 10]
            a[p, g + 8] = far[np.random.randint(len(far))]
    return np.exp2(a.ravel()).repeat(32)


def f64(x):
    return np.asarray(x).astype(np.float64)


def striped(idx):
    return np.tile(idx.reshape(-1, 16).T, (8, 1)).astype(np.uint16)


def unstriped(offs):
    return offs[:16].T.reshape(-1).astype(np.int64)


def pack_weight(w):
    k, n = w.shape
    w = f64(np.asarray(w, np.float32).astype(ml_dtypes.bfloat16)).reshape(k // 32, 32, n)
    amax = np.abs(w).max(1)
    byte = np.clip(np.where(amax > 0, np.frexp(amax)[1] - 1 + 127 - 7, 1), 1, 254)
    scaled = (w * np.exp2(127.0 - byte)[:, None, :]).reshape(k, n).astype(np.float32)
    words = np.ascontiguousarray(scaled.reshape(k // 512, 128, 4, n).transpose(0, 1, 3, 2)).astype(ml_dtypes.float8_e4m3fn).view(np.uint8)
    return words, np.ascontiguousarray(byte.astype(np.uint8).reshape(k // 512, 16, n))


def unpack_weight(words, scales):
    g, p, n, _ = words.shape
    vals = np.ascontiguousarray(words).view(ml_dtypes.float8_e4m3fn).astype(np.float64) * np.repeat(np.exp2(scales.astype(np.float64) - 127.0), 8, axis=1)[..., None]
    return vals.transpose(0, 1, 3, 2).reshape(g * 512, n)


def relu(v):
    return np.maximum(v, 0.0)


K, T, S, V, N = 1024, 1024, 512, 256, 128


def setup_inputs():
    n = np.random.standard_normal
    s = mx_kscale(K)[:, None]
    packed_w1 = pack_weight(n((K, N)) / np.sqrt(K) / s)
    packed_w2 = pack_weight(n((K, N)) / np.sqrt(K) / s)
    return {
        "xT": (n((K, T)) * s).astype(np.float32),
        "w1_words": packed_w1[0],
        "w1_scales": packed_w1[1],
        "w2_words": packed_w2[0],
        "w2_scales": packed_w2[1],
        "offs": striped(np.random.permutation(T)[:S]),
    }


def reference(xT, w1_words, w1_scales, w2_words, w2_scales, offs):
    xq = mxq(f64(xT)[:, unstriped(offs)], 0, "e4m3")
    e = np.exp(unpack_weight(w1_words, w1_scales).T @ xq)
    h = unpack_weight(w2_words, w2_scales).T @ xq
    num = e[:, :V] * h[:, :V] + e[:, V:2 * V] * h[:, V:2 * V]
    den = e[:, :V] + e[:, V:2 * V]
    return relu(num / den)

@@ -1,0 +1,129 @@
+from contextlib import ExitStack
+
+import concourse.mybir as mybir
+
+K, T, S, V, N = 1024, 1024, 512, 256, 128
+FLOPS = 2 * 2 * K * N * S
+
+F32 = mybir.dt.float32
+BF16 = mybir.dt.bfloat16
+I32 = mybir.dt.int32
+U32 = mybir.dt.uint32
+U16 = mybir.dt.uint16
+U8 = mybir.dt.uint8
+FP8X4 = mybir.dt.float8_e4m3fn_x4
+ALU = mybir.AluOpType
+ACT = mybir.ActivationFunctionType
+
+P = 128
+PASSES = K // 512
+LIST_ROWS = 16
+CHUNKS = (((0, 512, 320), (512, 1024, 320)), ((0, 512, 0), (512, 1024, 320)), ((0, 512, 0), (512, 1024, 160)), ((0, 512, 0), (512, 1024, 320)))
+SLICES = ((256, 256), (0, 128), (128, 128))
+WEAVE = {}
+
+
+def tile_picked_apool_relu_e_kernel(
+    tc, xT, w1_words, w1_scales, w2_words, w2_scales, offs, out
+):
+    nc = tc.nc
+    with ExitStack() as ctx:
+        keep = ctx.enter_context(tc.tile_pool(name="keep", bufs=1))
+        psum = ctx.enter_context(tc.psum_pool(name="psum", bufs=1))
+
+        offsets = keep.tile([P, S // LIST_ROWS], U16, name="offsets")
+        x_pairs = xT.rearrange("(z p u e) t -> z u p e t", z=PASSES, p=P, u=2, e=2)
+        raw = {}
+        for z in range(PASSES):
+            for u in range(2):
+                for t0, t1, cut in CHUNKS[2 * z + u]:
+                    raw[z, u, t0] = keep.tile([P, 2, t1 - t0], F32, name=f"raw{z}{u}{t0}")
+                    nc.sync.dma_start(out=raw[z, u, t0][:], in_=x_pairs[z, u][:, :, t0:t1])
+                    if (z, u, t0) == (0, 0, 0):
+                        nc.sync.dma_start(offsets[:], offs)
+
+        w_codes, w_scales = [], []
+        for i, words in enumerate((w1_words, w2_words)):
+            codes = keep.tile([P, PASSES, N], U32, name=f"w_codes{i}", align_bytes=64)
+            nc.sync.dma_start(
+                out=codes[:].bitcast(I32), in_=words.rearrange("z p n t -> p z (n t)").bitcast(I32)
+            )
+            w_codes.append(codes)
+        for i, (rows, queue) in enumerate(((w1_scales, nc.gpsimd), (w2_scales, nc.sync))):
+            plane = keep.tile([P, N], U8, name=f"w_scales{i}", align_bytes=64)
+            nc.gpsimd.memset(plane[:].bitcast(I32), 0)
+            for q in range(4):
+                queue.dma_start(
+                    out=plane[32 * q : 32 * q + 4 * PASSES, :].bitcast(I32),
+                    in_=rows[:, 4 * q : 4 * q + 4, :].bitcast(I32),
+                )
+            w_scales.append(plane)
+
+        score = {a: psum.tile([P, n], F32, name=f"score{a}") for a, n in SLICES}
+        value = {a: psum.tile([P, n], F32, name=f"value{a}") for a, n in SLICES}
+        probes = []
+
+        def round_pairs(z, u):
+            window = keep.tile([P, T, 2], BF16, name=f"window{z}{u}")
+            for t0, t1, cut in CHUNKS[2 * z + u]:
+                src = raw[z, u, t0][:].rearrange("p e t -> p t e")
+                if t0 + cut < t1:
+                    nc.scalar.activation(window[:, t0 + cut : t1, :], src[:, cut:, :], ACT.Copy)
+                if cut:
+                    nc.vector.tensor_copy(window[:, t0 : t0 + cut, :], src[:, :cut, :])
+            return window[:].rearrange("p t e -> p (t e)").bitcast(U32)
+
+        for z in range(PASSES):
+            grouped = {a: keep.tile([P, n, 2], U32, name=f"grouped{z}{a}", align_bytes=64) for a, n in SLICES}
+            picked = {a: keep.tile([P, 2, n], U32, name=f"picked{z}{a}") for a, n in SLICES if (z, a) in WEAVE}
+            for u in range(2):
+                window = round_pairs(z, u)
+                probes.append(window[:, 0:1].bitcast(I32))
+                for a, n in SLICES:
+                    cols = slice(a // LIST_ROWS, (a + n) // LIST_ROWS)
+                    target = picked[a][:, u, :] if (z, a) in WEAVE else grouped[a][:, :, u]
+                    nc.vector.tensor_copy(target, window.indirect(offsets[:, cols]))
+            for a, n in SLICES:
+                if WEAVE.get((z, a)) == "v":
+                    nc.vector.tensor_copy(grouped[a][:].bitcast(I32), picked[a][:].bitcast(I32).rearrange("p u v -> p v u"))
+                if WEAVE.get((z, a)) == "s":
+                    nc.scalar.copy(grouped[a][:], picked[a][:].rearrange("p u v -> p v u"))
+                codes = keep.tile([P, n], U32, name=f"x_codes{z}{a}", align_bytes=64)
+                scales = keep.tile([P, n], U8, name=f"x_scales{z}{a}", align_bytes=64)
+                nc.vector.quantize_mx(
+                    out=codes[:].bitcast(FP8X4),
+                    scales=scales[:],
+                    in_=grouped[a][:].rearrange("p v u -> p (v u)").bitcast(BF16),
+                )
+                probes.append(codes[:, 0:1].bitcast(I32))
+                for i, acc in enumerate((score[a], value[a])):
+                    nc.tensor.matmul_mx(
+                        out=acc[:],
+                        lhsT=w_codes[i][:, z, :].bitcast(FP8X4),
+                        lhsT_scale=w_scales[i][4 * z :, :],
+                        rhs=codes[:].bitcast(FP8X4),
+                        rhs_scale=scales[:],
+                        start=(z == 0),
+                        stop=(z == PASSES - 1),
+                    )
+
+        score1 = keep.tile([P, V], F32)
+        value1 = keep.tile([P, V], F32)
+        for a, n in SLICES:
+            if a >= V:
+                nc.scalar.copy(score1[:, a - V : a - V + n], score[a][:])
+                nc.scalar.copy(value1[:, a - V : a - V + n], value[a][:])
+        firsts = [(a, n) for a, n in SLICES if a < V]
+        names = ("score_gap", "value_gap", "tanh", "moved", "pooled", "result")
+        t = {(name, a): keep.tile([P, n], F32, name=f"{name}{a}") for name in names for a, n in firsts}
+        for a, n in firsts:
+            nc.vector.tensor_tensor(t["score_gap", a][:], score[a][:], score1[:, a : a + n], ALU.subtract)
+            nc.scalar.activation(t["tanh", a][:], t["score_gap", a][:], ACT.Tanh, scale=0.5)
+            nc.vector.tensor_tensor(t["value_gap", a][:], value[a][:], value1[:, a : a + n], ALU.subtract)
+        for a, n in firsts:
+            nc.vector.scalar_tensor_tensor(t["moved", a][:], t["tanh", a][:], 1.0, t["value_gap", a][:], ALU.add, ALU.mult)
+        for a, n in firsts:
+            nc.vector.scalar_tensor_tensor(t["pooled", a][:], t["moved", a][:], 0.5, value1[:, a : a + n], ALU.mult, ALU.add)
+        for a, n in firsts:
+            nc.vector.tensor_scalar_max(t["result", a][:], t["pooled", a][:], 0.0)
+            nc.sync.dma_start(out=out[:, a : a + n], in_=t["result", a][:])

@@ -18,9 +18,9 @@ ACT = mybir.ActivationFunctionType
 P = 128
 PASSES = K // 512
 LIST_ROWS = 16
-CHUNKS = (((0, 512, 320), (512, 1024, 320)), ((0, 512, 0), (512, 1024, 320)), ((0, 512, 0), (512, 1024, 160)), ((0, 512, 0), (512, 1024, 320)))
+CHUNKS = (((0, 512, 320), (512, 1024, 320)), ((0, 512, 0), (512, 1024, 320)), ((0, 512, 0), (512, 1024, 0)), ((0, 512, 0), (512, 1024, 192)))
 SLICES = ((256, 256), (0, 128), (128, 128))
-WEAVE = {}
+WEAVE = {(0, 256): "v", (0, 0): "v", (1, 256): "step", (1, 0): "s", (1, 128): "s"}
 
 
 def tile_picked_apool_relu_e_kernel(
@@ -35,29 +35,29 @@ def tile_picked_apool_relu_e_kernel(
         x_pairs = xT.rearrange("(z p u e) t -> z u p e t", z=PASSES, p=P, u=2, e=2)
         raw = {}
         for z in range(PASSES):
-            for u in range(2):
-                for t0, t1, cut in CHUNKS[2 * z + u]:
+            for u in (1, 0):
+                for t0, t1, cut in CHUNKS[2 * z + 1 - u]:
                     raw[z, u, t0] = keep.tile([P, 2, t1 - t0], F32, name=f"raw{z}{u}{t0}")
                     nc.sync.dma_start(out=raw[z, u, t0][:], in_=x_pairs[z, u][:, :, t0:t1])
-                    if (z, u, t0) == (0, 0, 0):
+                    if (z, u, t0) == (0, 1, 0):
                         nc.sync.dma_start(offsets[:], offs)
 
-        w_codes, w_scales = [], []
+        w_codes = []
         for i, words in enumerate((w1_words, w2_words)):
             codes = keep.tile([P, PASSES, N], U32, name=f"w_codes{i}", align_bytes=64)
             nc.sync.dma_start(
                 out=codes[:].bitcast(I32), in_=words.rearrange("z p n t -> p z (n t)").bitcast(I32)
             )
             w_codes.append(codes)
+        w_scales = keep.tile([P, N], U8, name="w_scales", align_bytes=64)
+        nc.gpsimd.memset(w_scales[:].bitcast(I32), 0)
         for i, (rows, queue) in enumerate(((w1_scales, nc.gpsimd), (w2_scales, nc.sync))):
-            plane = keep.tile([P, N], U8, name=f"w_scales{i}", align_bytes=64)
-            nc.gpsimd.memset(plane[:].bitcast(I32), 0)
             for q in range(4):
+                first = 32 * q + 8 * i
                 queue.dma_start(
-                    out=plane[32 * q : 32 * q + 4 * PASSES, :].bitcast(I32),
+                    out=w_scales[first : first + 8, :].bitcast(I32),
                     in_=rows[:, 4 * q : 4 * q + 4, :].bitcast(I32),
                 )
-            w_scales.append(plane)
 
         score = {a: psum.tile([P, n], F32, name=f"score{a}") for a, n in SLICES}
         value = {a: psum.tile([P, n], F32, name=f"value{a}") for a, n in SLICES}
@@ -65,7 +65,7 @@ def tile_picked_apool_relu_e_kernel(
 
         def round_pairs(z, u):
             window = keep.tile([P, T, 2], BF16, name=f"window{z}{u}")
-            for t0, t1, cut in CHUNKS[2 * z + u]:
+            for t0, t1, cut in CHUNKS[2 * z + 1 - u]:
                 src = raw[z, u, t0][:].rearrange("p e t -> p t e")
                 if t0 + cut < t1:
                     nc.scalar.activation(window[:, t0 + cut : t1, :], src[:, cut:, :], ACT.Copy)
@@ -74,20 +74,35 @@ def tile_picked_apool_relu_e_kernel(
             return window[:].rearrange("p t e -> p (t e)").bitcast(U32)
 
         for z in range(PASSES):
-            grouped = {a: keep.tile([P, n, 2], U32, name=f"grouped{z}{a}", align_bytes=64) for a, n in SLICES}
-            picked = {a: keep.tile([P, 2, n], U32, name=f"picked{z}{a}") for a, n in SLICES if (z, a) in WEAVE}
-            for u in range(2):
+            parts = SLICES if z == 1 else ((V, V), (0, V))
+            grouped = {a: keep.tile([P, n, 2], U32, name=f"grouped{z}{a}", align_bytes=64) for a, n in parts}
+            picked = keep.tile([P, 2, S], U32, name=f"picked{z}")
+            stepped = [(a, n) for a, n in parts if WEAVE[z, a] == "step"]
+
+            def weave(a, n):
+                if WEAVE[z, a] == "s":
+                    nc.scalar.copy(grouped[a][:], picked[:, :, a : a + n].rearrange("p u v -> p v u"))
+                if WEAVE[z, a] == "v":
+                    nc.vector.tensor_copy(
+                        grouped[a][:].bitcast(I32), picked[:].bitcast(I32)[:, :, a : a + n].rearrange("p u v -> p v u")
+                    )
+
+            for u in (1, 0):
                 window = round_pairs(z, u)
-                probes.append(window[:, 0:1].bitcast(I32))
-                for a, n in SLICES:
+                if (z, u) == (1, 0):
+                    cuts = SLICES
+                else:
+                    cuts = ((V, V), (0, V)) if stepped else ((0, S),)
+                for j, (a, n) in enumerate(cuts):
                     cols = slice(a // LIST_ROWS, (a + n) // LIST_ROWS)
-                    target = picked[a][:, u, :] if (z, a) in WEAVE else grouped[a][:, :, u]
+                    target = grouped[a][:, :, u] if (a, n) in stepped else picked[:, u, a : a + n]
                     nc.vector.tensor_copy(target, window.indirect(offsets[:, cols]))
-            for a, n in SLICES:
-                if WEAVE.get((z, a)) == "v":
-                    nc.vector.tensor_copy(grouped[a][:].bitcast(I32), picked[a][:].bitcast(I32).rearrange("p u v -> p v u"))
-                if WEAVE.get((z, a)) == "s":
-                    nc.scalar.copy(grouped[a][:], picked[a][:].rearrange("p u v -> p v u"))
+                    if (z, u, j) == (1, 0, 1):
+                        weave(V, V)
+            for a, n in parts:
+                if (z, a) != (1, V):
+                    weave(a, n)
+            for a, n in parts:
                 codes = keep.tile([P, n], U32, name=f"x_codes{z}{a}", align_bytes=64)
                 scales = keep.tile([P, n], U8, name=f"x_scales{z}{a}", align_bytes=64)
                 nc.vector.quantize_mx(
@@ -96,16 +111,18 @@ def tile_picked_apool_relu_e_kernel(
                     in_=grouped[a][:].rearrange("p v u -> p (v u)").bitcast(BF16),
                 )
                 probes.append(codes[:, 0:1].bitcast(I32))
-                for i, acc in enumerate((score[a], value[a])):
-                    nc.tensor.matmul_mx(
-                        out=acc[:],
-                        lhsT=w_codes[i][:, z, :].bitcast(FP8X4),
-                        lhsT_scale=w_scales[i][4 * z :, :],
-                        rhs=codes[:].bitcast(FP8X4),
-                        rhs_scale=scales[:],
-                        start=(z == 0),
-                        stop=(z == PASSES - 1),
-                    )
+                for b, m in SLICES:
+                    if a <= b < a + n:
+                        for i, acc in enumerate((score[b], value[b])):
+                            nc.tensor.matmul_mx(
+                                out=acc[:],
+                                lhsT=w_codes[i][:, z, :].bitcast(FP8X4),
+                                lhsT_scale=w_scales[8 * i + 4 * z :, :],
+                                rhs=codes[:, b - a : b - a + m].bitcast(FP8X4),
+                                rhs_scale=scales[:, b - a : b - a + m],
+                                start=(z == 0),
+                                stop=(z == PASSES - 1),
+                            )
 
         score1 = keep.tile([P, V], F32)
         value1 = keep.tile([P, V], F32)

@@ -17,10 +17,27 @@ ACT = mybir.ActivationFunctionType
 
 P = 128
 PASSES = K // 512
-LIST_ROWS = 16
-CHUNKS = (((0, 512, 320), (512, 1024, 320)), ((0, 512, 0), (512, 1024, 320)), ((0, 512, 0), (512, 1024, 0)), ((0, 512, 0), (512, 1024, 192)))
-SLICES = ((256, 256), (0, 128), (128, 128))
-WEAVE = {(0, 256): "v", (0, 0): "v", (1, 256): "step", (1, 0): "s", (1, 128): "s"}
+PER_COLUMN = 16
+CHUNK = 512
+QUADRANT = 32
+SCALE_ROWS = 4
+
+PAIRS = tuple((z, u) for z in range(PASSES) for u in (1, 0))
+LAST_PAIR = PAIRS[-1]
+
+SECONDS = (V, V)
+FIRSTS = (0, V)
+FIRST_HALVES = ((0, V // 2), (V // 2, V // 2))
+SPANS = (SECONDS,) + FIRST_HALVES
+
+SHARE_IDLE = 320
+SHARE_LAST = 288
+VECTOR_SHARES = {
+    PAIRS[0]: (SHARE_IDLE, SHARE_IDLE),
+    PAIRS[1]: (0, SHARE_IDLE),
+    PAIRS[2]: (0, 0),
+    PAIRS[3]: (0, SHARE_LAST),
+}
 
 
 def tile_picked_apool_relu_e_kernel(
@@ -31,116 +48,112 @@ def tile_picked_apool_relu_e_kernel(
         keep = ctx.enter_context(tc.tile_pool(name="keep", bufs=1))
         psum = ctx.enter_context(tc.psum_pool(name="psum", bufs=1))
 
-        offsets = keep.tile([P, S // LIST_ROWS], U16, name="offsets")
+        offsets = keep.tile([P, S // PER_COLUMN], U16, name="offsets")
         x_pairs = xT.rearrange("(z p u e) t -> z u p e t", z=PASSES, p=P, u=2, e=2)
         raw = {}
-        for z in range(PASSES):
-            for u in (1, 0):
-                for t0, t1, cut in CHUNKS[2 * z + 1 - u]:
-                    raw[z, u, t0] = keep.tile([P, 2, t1 - t0], F32, name=f"raw{z}{u}{t0}")
-                    nc.sync.dma_start(out=raw[z, u, t0][:], in_=x_pairs[z, u][:, :, t0:t1])
-                    if (z, u, t0) == (0, 1, 0):
-                        nc.sync.dma_start(offsets[:], offs)
+        for z, u in PAIRS:
+            for t0 in range(0, T, CHUNK):
+                raw[z, u, t0] = keep.tile([P, 2, CHUNK], F32, name=f"raw{z}{u}{t0}")
+                nc.sync.dma_start(out=raw[z, u, t0][:], in_=x_pairs[z, u][:, :, t0 : t0 + CHUNK])
+                if (z, u) == PAIRS[0] and t0 == 0:
+                    nc.sync.dma_start(offsets[:], offs)
 
         w_codes = []
         for i, words in enumerate((w1_words, w2_words)):
-            codes = keep.tile([P, PASSES, N], U32, name=f"w_codes{i}", align_bytes=64)
+            w_tile = keep.tile([P, PASSES, N], U32, name=f"w_codes{i}", align_bytes=64)
             nc.sync.dma_start(
-                out=codes[:].bitcast(I32), in_=words.rearrange("z p n t -> p z (n t)").bitcast(I32)
+                out=w_tile[:].bitcast(I32), in_=words.rearrange("z p n t -> p z (n t)").bitcast(I32)
             )
-            w_codes.append(codes)
+            w_codes.append(w_tile)
+
         w_scales = keep.tile([P, N], U8, name="w_scales", align_bytes=64)
         nc.gpsimd.memset(w_scales[:].bitcast(I32), 0)
-        for i, (rows, queue) in enumerate(((w1_scales, nc.gpsimd), (w2_scales, nc.sync))):
-            for q in range(4):
-                first = 32 * q + 8 * i
+        rows_per_weight = PASSES * SCALE_ROWS
+        for i, (rows, queue) in enumerate(((w1_scales, nc.gpsimd), (w2_scales, nc.gpsimd))):
+            for q in range(P // QUADRANT):
+                first = QUADRANT * q + rows_per_weight * i
                 queue.dma_start(
-                    out=w_scales[first : first + 8, :].bitcast(I32),
-                    in_=rows[:, 4 * q : 4 * q + 4, :].bitcast(I32),
+                    out=w_scales[first : first + rows_per_weight, :].bitcast(I32),
+                    in_=rows[:, SCALE_ROWS * q : SCALE_ROWS * (q + 1), :].bitcast(I32),
                 )
 
-        score = {a: psum.tile([P, n], F32, name=f"score{a}") for a, n in SLICES}
-        value = {a: psum.tile([P, n], F32, name=f"value{a}") for a, n in SLICES}
-        probes = []
+        score = {a: psum.tile([P, n], F32, name=f"score{a}") for a, n in SPANS}
+        value = {a: psum.tile([P, n], F32, name=f"value{a}") for a, n in SPANS}
 
-        def round_pairs(z, u):
+        def round_pair(z, u):
             window = keep.tile([P, T, 2], BF16, name=f"window{z}{u}")
-            for t0, t1, cut in CHUNKS[2 * z + 1 - u]:
+            for t0, share in zip(range(0, T, CHUNK), VECTOR_SHARES[z, u]):
                 src = raw[z, u, t0][:].rearrange("p e t -> p t e")
-                if t0 + cut < t1:
-                    nc.scalar.activation(window[:, t0 + cut : t1, :], src[:, cut:, :], ACT.Copy)
-                if cut:
-                    nc.vector.tensor_copy(window[:, t0 : t0 + cut, :], src[:, :cut, :])
+                nc.scalar.activation(window[:, t0 + share : t0 + CHUNK, :], src[:, share:, :], ACT.Copy)
+                if share:
+                    nc.vector.tensor_copy(window[:, t0 : t0 + share, :], src[:, :share, :])
             return window[:].rearrange("p t e -> p (t e)").bitcast(U32)
 
-        for z in range(PASSES):
-            parts = SLICES if z == 1 else ((V, V), (0, V))
-            grouped = {a: keep.tile([P, n, 2], U32, name=f"grouped{z}{a}", align_bytes=64) for a, n in parts}
-            picked = keep.tile([P, 2, S], U32, name=f"picked{z}")
-            stepped = [(a, n) for a, n in parts if WEAVE[z, a] == "step"]
+        def gather(target, window, a, n):
+            columns = offsets[:, a // PER_COLUMN : (a + n) // PER_COLUMN]
+            nc.vector.tensor_copy(target, window.indirect(columns))
 
-            def weave(a, n):
-                if WEAVE[z, a] == "s":
-                    nc.scalar.copy(grouped[a][:], picked[:, :, a : a + n].rearrange("p u v -> p v u"))
-                if WEAVE[z, a] == "v":
-                    nc.vector.tensor_copy(
-                        grouped[a][:].bitcast(I32), picked[:].bitcast(I32)[:, :, a : a + n].rearrange("p u v -> p v u")
-                    )
+        def multiply(z, grouped, a, n):
+            codes = keep.tile([P, n], U32, name=f"x_codes{z}{a}", align_bytes=64)
+            scales = keep.tile([P, n], U8, name=f"x_scales{z}{a}", align_bytes=64)
+            nc.vector.quantize_mx(
+                out=codes[:].bitcast(FP8X4),
+                scales=scales[:],
+                in_=grouped[:].rearrange("p v u -> p (v u)").bitcast(BF16),
+            )
+            for b, m in SPANS:
+                if a <= b < a + n:
+                    for i, acc in enumerate((score[b], value[b])):
+                        nc.tensor.matmul_mx(
+                            out=acc[:],
+                            lhsT=w_codes[i][:, z, :].bitcast(FP8X4),
+                            lhsT_scale=w_scales[rows_per_weight * i + SCALE_ROWS * z :, :],
+                            rhs=codes[:, b - a : b - a + m].bitcast(FP8X4),
+                            rhs_scale=scales[:, b - a : b - a + m],
+                            start=(z == 0),
+                            stop=(z == PASSES - 1),
+                        )
 
-            for u in (1, 0):
-                window = round_pairs(z, u)
-                if (z, u) == (1, 0):
-                    cuts = SLICES
-                else:
-                    cuts = ((V, V), (0, V)) if stepped else ((0, S),)
-                for j, (a, n) in enumerate(cuts):
-                    cols = slice(a // LIST_ROWS, (a + n) // LIST_ROWS)
-                    target = grouped[a][:, :, u] if (a, n) in stepped else picked[:, u, a : a + n]
-                    nc.vector.tensor_copy(target, window.indirect(offsets[:, cols]))
-                    if (z, u, j) == (1, 0, 1):
-                        weave(V, V)
-            for a, n in parts:
-                if (z, a) != (1, V):
-                    weave(a, n)
-            for a, n in parts:
-                codes = keep.tile([P, n], U32, name=f"x_codes{z}{a}", align_bytes=64)
-                scales = keep.tile([P, n], U8, name=f"x_scales{z}{a}", align_bytes=64)
-                nc.vector.quantize_mx(
-                    out=codes[:].bitcast(FP8X4),
-                    scales=scales[:],
-                    in_=grouped[a][:].rearrange("p v u -> p (v u)").bitcast(BF16),
-                )
-                probes.append(codes[:, 0:1].bitcast(I32))
-                for b, m in SLICES:
-                    if a <= b < a + n:
-                        for i, acc in enumerate((score[b], value[b])):
-                            nc.tensor.matmul_mx(
-                                out=acc[:],
-                                lhsT=w_codes[i][:, z, :].bitcast(FP8X4),
-                                lhsT_scale=w_scales[8 * i + 4 * z :, :],
-                                rhs=codes[:, b - a : b - a + m].bitcast(FP8X4),
-                                rhs_scale=scales[:, b - a : b - a + m],
-                                start=(z == 0),
-                                stop=(z == PASSES - 1),
-                            )
+        grouped = {a: keep.tile([P, n, 2], U32, name=f"grouped0{a}", align_bytes=64) for a, n in (SECONDS, FIRSTS)}
+        picked = keep.tile([P, 2, S], U32, name="picked0")
+        for u in (1, 0):
+            gather(picked[:, u, :], round_pair(0, u), 0, S)
+        for a, n in (SECONDS, FIRSTS):
+            words = picked[:].bitcast(I32)[:, :, a : a + n]
+            nc.vector.tensor_copy(grouped[a][:].bitcast(I32), words.rearrange("p u v -> p v u"))
+        for a, n in (SECONDS, FIRSTS):
+            multiply(0, grouped[a], a, n)
+
+        grouped = {a: keep.tile([P, n, 2], U32, name=f"grouped1{a}", align_bytes=64) for a, n in SPANS}
+        picked = keep.tile([P, 2, V], U32, name="picked1")
+        for u in (1, 0):
+            window = round_pair(1, u)
+            gather(grouped[V][:, :, u], window, *SECONDS)
+            for a, n in FIRST_HALVES if (1, u) == LAST_PAIR else (FIRSTS,):
+                gather(picked[:, u, a : a + n], window, a, n)
+        for a, n in FIRST_HALVES:
+            nc.scalar.copy(grouped[a][:], picked[:, :, a : a + n].rearrange("p u v -> p v u"))
+        for a, n in SPANS:
+            multiply(1, grouped[a], a, n)
 
         score1 = keep.tile([P, V], F32)
         value1 = keep.tile([P, V], F32)
-        for a, n in SLICES:
-            if a >= V:
-                nc.scalar.copy(score1[:, a - V : a - V + n], score[a][:])
-                nc.scalar.copy(value1[:, a - V : a - V + n], value[a][:])
-        firsts = [(a, n) for a, n in SLICES if a < V]
-        names = ("score_gap", "value_gap", "tanh", "moved", "pooled", "result")
-        t = {(name, a): keep.tile([P, n], F32, name=f"{name}{a}") for name in names for a, n in firsts}
-        for a, n in firsts:
-            nc.vector.tensor_tensor(t["score_gap", a][:], score[a][:], score1[:, a : a + n], ALU.subtract)
-            nc.scalar.activation(t["tanh", a][:], t["score_gap", a][:], ACT.Tanh, scale=0.5)
-            nc.vector.tensor_tensor(t["value_gap", a][:], value[a][:], value1[:, a : a + n], ALU.subtract)
-        for a, n in firsts:
-            nc.vector.scalar_tensor_tensor(t["moved", a][:], t["tanh", a][:], 1.0, t["value_gap", a][:], ALU.add, ALU.mult)
-        for a, n in firsts:
-            nc.vector.scalar_tensor_tensor(t["pooled", a][:], t["moved", a][:], 0.5, value1[:, a : a + n], ALU.mult, ALU.add)
-        for a, n in firsts:
-            nc.vector.tensor_scalar_max(t["result", a][:], t["pooled", a][:], 0.0)
-            nc.sync.dma_start(out=out[:, a : a + n], in_=t["result", a][:])
+        nc.scalar.copy(score1[:], score[V][:])
+        nc.scalar.copy(value1[:], value[V][:])
+
+        def half_tiles(name):
+            return {a: keep.tile([P, n], F32, name=f"{name}{a}") for a, n in FIRST_HALVES}
+
+        score_gap, value_gap, tanh = half_tiles("score_gap"), half_tiles("value_gap"), half_tiles("tanh")
+        moved, pooled, result = half_tiles("moved"), half_tiles("pooled"), half_tiles("result")
+        for a, n in FIRST_HALVES:
+            nc.vector.tensor_tensor(score_gap[a][:], score[a][:], score1[:, a : a + n], ALU.subtract)
+            nc.scalar.activation(tanh[a][:], score_gap[a][:], ACT.Tanh, scale=0.5)
+            nc.vector.tensor_tensor(value_gap[a][:], value[a][:], value1[:, a : a + n], ALU.subtract)
+        for a, n in FIRST_HALVES:
+            nc.vector.scalar_tensor_tensor(moved[a][:], tanh[a][:], 1.0, value_gap[a][:], ALU.add, ALU.mult)
+        for a, n in FIRST_HALVES:
+            nc.vector.scalar_tensor_tensor(pooled[a][:], moved[a][:], 0.5, value1[:, a : a + n], ALU.mult, ALU.add)
+        for a, n in FIRST_HALVES:
+            nc.vector.tensor_scalar_max(result[a][:], pooled[a][:], 0.0)
+            nc.sync.dma_start(out=out[:, a : a + n], in_=result[a][:])

from contextlib import ExitStack

import concourse.mybir as mybir

K, T, S, V, N = 1024, 1024, 512, 256, 128
FLOPS = 2 * 2 * K * N * S

F32 = mybir.dt.float32
BF16 = mybir.dt.bfloat16
I32 = mybir.dt.int32
U32 = mybir.dt.uint32
U16 = mybir.dt.uint16
U8 = mybir.dt.uint8
FP8X4 = mybir.dt.float8_e4m3fn_x4
ALU = mybir.AluOpType
ACT = mybir.ActivationFunctionType

P = 128
PASSES = K // 512
PER_COLUMN = 16
CHUNK = 512
QUADRANT = 32
SCALE_ROWS = 4

PAIRS = tuple((z, u) for z in range(PASSES) for u in (1, 0))
LAST_PAIR = PAIRS[-1]

SECONDS = (V, V)
FIRSTS = (0, V)
FIRST_HALVES = ((0, V // 2), (V // 2, V // 2))
SPANS = (SECONDS,) + FIRST_HALVES

SHARE_IDLE = 320
SHARE_LAST = 288
VECTOR_SHARES = {
    PAIRS[0]: (SHARE_IDLE, SHARE_IDLE),
    PAIRS[1]: (0, SHARE_IDLE),
    PAIRS[2]: (0, 0),
    PAIRS[3]: (0, SHARE_LAST),
}


def tile_picked_apool_relu_e_kernel(
    tc, xT, w1_words, w1_scales, w2_words, w2_scales, offs, out
):
    nc = tc.nc
    with ExitStack() as ctx:
        keep = ctx.enter_context(tc.tile_pool(name="keep", bufs=1))
        psum = ctx.enter_context(tc.psum_pool(name="psum", bufs=1))

        offsets = keep.tile([P, S // PER_COLUMN], U16, name="offsets")
        x_pairs = xT.rearrange("(z p u e) t -> z u p e t", z=PASSES, p=P, u=2, e=2)
        raw = {}
        for z, u in PAIRS:
            for t0 in range(0, T, CHUNK):
                raw[z, u, t0] = keep.tile([P, 2, CHUNK], F32, name=f"raw{z}{u}{t0}")
                nc.sync.dma_start(out=raw[z, u, t0][:], in_=x_pairs[z, u][:, :, t0 : t0 + CHUNK])
                if (z, u) == PAIRS[0] and t0 == 0:
                    nc.sync.dma_start(offsets[:], offs)

        w_codes = []
        for i, words in enumerate((w1_words, w2_words)):
            w_tile = keep.tile([P, PASSES, N], U32, name=f"w_codes{i}", align_bytes=64)
            nc.sync.dma_start(
                out=w_tile[:].bitcast(I32), in_=words.rearrange("z p n t -> p z (n t)").bitcast(I32)
            )
            w_codes.append(w_tile)

        w_scales = keep.tile([P, N], U8, name="w_scales", align_bytes=64)
        nc.gpsimd.memset(w_scales[:].bitcast(I32), 0)
        rows_per_weight = PASSES * SCALE_ROWS
        for i, (rows, queue) in enumerate(((w1_scales, nc.gpsimd), (w2_scales, nc.gpsimd))):
            for q in range(P // QUADRANT):
                first = QUADRANT * q + rows_per_weight * i
                queue.dma_start(
                    out=w_scales[first : first + rows_per_weight, :].bitcast(I32),
                    in_=rows[:, SCALE_ROWS * q : SCALE_ROWS * (q + 1), :].bitcast(I32),
                )

        score = {a: psum.tile([P, n], F32, name=f"score{a}") for a, n in SPANS}
        value = {a: psum.tile([P, n], F32, name=f"value{a}") for a, n in SPANS}

        def round_pair(z, u):
            window = keep.tile([P, T, 2], BF16, name=f"window{z}{u}")
            for t0, share in zip(range(0, T, CHUNK), VECTOR_SHARES[z, u]):
                src = raw[z, u, t0][:].rearrange("p e t -> p t e")
                nc.scalar.activation(window[:, t0 + share : t0 + CHUNK, :], src[:, share:, :], ACT.Copy)
                if share:
                    nc.vector.tensor_copy(window[:, t0 : t0 + share, :], src[:, :share, :])
            return window[:].rearrange("p t e -> p (t e)").bitcast(U32)

        def gather(target, window, a, n):
            columns = offsets[:, a // PER_COLUMN : (a + n) // PER_COLUMN]
            nc.vector.tensor_copy(target, window.indirect(columns))

        def multiply(z, grouped, a, n):
            codes = keep.tile([P, n], U32, name=f"x_codes{z}{a}", align_bytes=64)
            scales = keep.tile([P, n], U8, name=f"x_scales{z}{a}", align_bytes=64)
            nc.vector.quantize_mx(
                out=codes[:].bitcast(FP8X4),
                scales=scales[:],
                in_=grouped[:].rearrange("p v u -> p (v u)").bitcast(BF16),
            )
            for b, m in SPANS:
                if a <= b < a + n:
                    for i, acc in enumerate((score[b], value[b])):
                        nc.tensor.matmul_mx(
                            out=acc[:],
                            lhsT=w_codes[i][:, z, :].bitcast(FP8X4),
                            lhsT_scale=w_scales[rows_per_weight * i + SCALE_ROWS * z :, :],
                            rhs=codes[:, b - a : b - a + m].bitcast(FP8X4),
                            rhs_scale=scales[:, b - a : b - a + m],
                            start=(z == 0),
                            stop=(z == PASSES - 1),
                        )

        grouped = {a: keep.tile([P, n, 2], U32, name=f"grouped0{a}", align_bytes=64) for a, n in (SECONDS, FIRSTS)}
        picked = keep.tile([P, 2, S], U32, name="picked0")
        for u in (1, 0):
            gather(picked[:, u, :], round_pair(0, u), 0, S)
        for a, n in (SECONDS, FIRSTS):
            words = picked[:].bitcast(I32)[:, :, a : a + n]
            nc.vector.tensor_copy(grouped[a][:].bitcast(I32), words.rearrange("p u v -> p v u"))
        for a, n in (SECONDS, FIRSTS):
            multiply(0, grouped[a], a, n)

        grouped = {a: keep.tile([P, n, 2], U32, name=f"grouped1{a}", align_bytes=64) for a, n in SPANS}
        picked = keep.tile([P, 2, V], U32, name="picked1")
        for u in (1, 0):
            window = round_pair(1, u)
            gather(grouped[V][:, :, u], window, *SECONDS)
            for a, n in FIRST_HALVES if (1, u) == LAST_PAIR else (FIRSTS,):
                gather(picked[:, u, a : a + n], window, a, n)
        for a, n in FIRST_HALVES:
            nc.scalar.copy(grouped[a][:], picked[:, :, a : a + n].rearrange("p u v -> p v u"))
        for a, n in SPANS:
            multiply(1, grouped[a], a, n)

        score1 = keep.tile([P, V], F32)
        value1 = keep.tile([P, V], F32)
        nc.scalar.copy(score1[:], score[V][:])
        nc.scalar.copy(value1[:], value[V][:])

        def half_tiles(name):
            return {a: keep.tile([P, n], F32, name=f"{name}{a}") for a, n in FIRST_HALVES}

        score_gap, value_gap, tanh = half_tiles("score_gap"), half_tiles("value_gap"), half_tiles("tanh")
        moved, pooled, result = half_tiles("moved"), half_tiles("pooled"), half_tiles("result")
        for a, n in FIRST_HALVES:
            nc.vector.tensor_tensor(score_gap[a][:], score[a][:], score1[:, a : a + n], ALU.subtract)
            nc.scalar.activation(tanh[a][:], score_gap[a][:], ACT.Tanh, scale=0.5)
            nc.vector.tensor_tensor(value_gap[a][:], value[a][:], value1[:, a : a + n], ALU.subtract)
        for a, n in FIRST_HALVES:
            nc.vector.scalar_tensor_tensor(moved[a][:], tanh[a][:], 1.0, value_gap[a][:], ALU.add, ALU.mult)
        for a, n in FIRST_HALVES:
            nc.vector.scalar_tensor_tensor(pooled[a][:], moved[a][:], 0.5, value1[:, a : a + n], ALU.mult, ALU.add)
        for a, n in FIRST_HALVES:
            nc.vector.tensor_scalar_max(result[a][:], pooled[a][:], 0.0)
            nc.sync.dma_start(out=out[:, a : a + n], in_=result[a][:])
